import numpy as np
CORES = [2,6,18,22,34,38,50,54,66,70,82,86,98,102,114,118]
N = 16
GROUPS = [[0,2,4,6,8,10,12,14],[1,3,5,7,9,11,13,15]]
def setup_inputs(rng):
    return {"x": rng.standard_normal((N, 128, 256), dtype=np.float32)}
def reference(x):
    y = np.empty((N, 128, 32), x.dtype)
    for g in GROUPS:
        s = x[g].sum(axis=0, dtype=np.float64).astype(x[g].dtype)
        n = len(g); b = x.shape[2] // n
        for i, r in enumerate(g):
            y[r] = s[:, i * b:(i + 1) * b]
    return {"y": y}

@@ -1,0 +1,47 @@
+from concourse.mybir import AluOpType
+
+SCRATCH = {
+    "xs": ("sbuf", [128, 256], "float32"),
+    "land": ("sbuf", [128, 256], "float32"),
+}
+SEMAPHORES = ["loaded", "own", "sent", "arrived", "added"]
+
+
+def rank_program(g, core, T, topo):
+    rank = T.rank_of(core)
+    if rank is None:
+        return
+    group = [m for m in T.tables["GROUPS"] if rank in m][0]
+    n = len(group)
+    i = group.index(rank)
+    b = T.x.shape[1] // n
+    sem = T.sem
+
+    g.sync.dma_start(T.xs[:], T.x[:]).then_inc(sem.loaded, 16)
+    g.scalar.dma_start(T.land[:, i * b:(i + 1) * b], T.x[:, i * b:(i + 1) * b]).then_inc(sem.own, 16)
+    g.wait_ge(sem.loaded, 16)
+
+    engines = 0
+    for k in range(1, n):
+        j = (i + k) % n
+        dst = T.cores[group[j]]
+        rid, pid, _se = topo.addr(dst)
+        m = topo.mask(core, dst)
+        engines = bin(m).count("1")
+        g.remote_dma(T.land[:, i * b:(i + 1) * b], T.xs[:, j * b:(j + 1) * b],
+                     sem.arrived, sem.sent, pid, rid, m)
+
+    g.wait_ge(sem.own, 16)
+    g.wait_ge(sem.arrived, engines * (n - 1))
+    done = 0
+    w = n * b // 2
+    while w >= b:
+        g.dma_start(T.land[:, 0:w], T.land[:, w:2 * w], accum_op=AluOpType.add).then_inc(sem.added, 16)
+        done += 16
+        g.wait_ge(sem.added, done)
+        w //= 2
+
+    g.dma_start(T.y[:], T.land[:, 0:b]).then_inc(sem.added, 16)
+    done += 16
+    g.wait_ge(sem.added, done)
+    g.wait_ge(sem.sent, engines * (n - 1))

@@ -1,47 +1,61 @@
+from concourse.bass import DstId, RemoteDMATransfer
 from concourse.mybir import AluOpType
 
 SCRATCH = {
-    "xs": ("sbuf", [128, 256], "float32"),
-    "land": ("sbuf", [128, 256], "float32"),
+    "stage": ("dram", [8, 128, 32], "float32"),
+    "land": ("dram", [8, 128, 32], "float32"),
+    "res": ("dram", [128, 32], "float32"),
 }
-SEMAPHORES = ["loaded", "own", "sent", "arrived", "added"]
+SEMAPHORES = ["staged", "sent", "arrived", "folded", "mine"]
+
+
+def helper_of(c):
+    return c + 1
 
 
 def rank_program(g, core, T, topo):
+    sem = T.sem
+    groups = T.tables["GROUPS"]
     rank = T.rank_of(core)
+
     if rank is None:
+        owner = T.rank_of(core - 1) if core >= 1 else None
+        if owner is None or helper_of(core - 1) != core:
+            return
+        group = [m for m in groups if owner in m][0]
+        i = group.index(owner)
+        n = len(group)
+        g.wait_ge(sem.arrived, n - 1)
+        rid, pid, _se = topo.addr(core - 1)
+        m = topo.mask(core, core - 1)
+        g.remote_dma_fused(
+            [RemoteDMATransfer(dst_ids=[DstId(rid=rid, pnc=pid)], dma_engine_mask=m, remote_sem=sem.folded,
+                               srcs=[T.land[s] for s in range(n) if s != i], dsts=[T.res[:]], alu_op=1)],
+            local_sem=sem.sent)
+        g.wait_ge(sem.sent, bin(m).count("1"))
         return
-    group = [m for m in T.tables["GROUPS"] if rank in m][0]
+
+    group = [m for m in groups if rank in m][0]
     n = len(group)
     i = group.index(rank)
     b = T.x.shape[1] // n
-    sem = T.sem
 
-    g.sync.dma_start(T.xs[:], T.x[:]).then_inc(sem.loaded, 16)
-    g.scalar.dma_start(T.land[:, i * b:(i + 1) * b], T.x[:, i * b:(i + 1) * b]).then_inc(sem.own, 16)
-    g.wait_ge(sem.loaded, 16)
+    g.dma_start(T.y[:], T.x[:, i * b:(i + 1) * b]).then_inc(sem.mine, 16)
+    others = [(i + k) % n for k in range(1, n)]
+    for k, j in enumerate(others):
+        q = g.sync if k % 2 == 0 else g.scalar
+        q.dma_start(T.stage[j], T.x[:, j * b:(j + 1) * b]).then_inc(sem.staged, 16)
+    g.wait_ge(sem.staged, 16 * len(others))
 
-    engines = 0
-    for k in range(1, n):
-        j = (i + k) % n
-        dst = T.cores[group[j]]
-        rid, pid, _se = topo.addr(dst)
-        m = topo.mask(core, dst)
-        engines = bin(m).count("1")
-        g.remote_dma(T.land[:, i * b:(i + 1) * b], T.xs[:, j * b:(j + 1) * b],
-                     sem.arrived, sem.sent, pid, rid, m)
+    transfers = []
+    for k, j in enumerate(others):
+        rid, pid, _se = topo.addr(helper_of(T.cores[group[j]]))
+        transfers.append(RemoteDMATransfer(dst_ids=[DstId(rid=rid, pnc=pid)], dma_engine_mask=1 << k,
+                                           remote_sem=sem.arrived, src=T.stage[j], dst=T.land[i]))
+    g.remote_dma_fused(transfers, local_sem=sem.sent)
 
-    g.wait_ge(sem.own, 16)
-    g.wait_ge(sem.arrived, engines * (n - 1))
-    done = 0
-    w = n * b // 2
-    while w >= b:
-        g.dma_start(T.land[:, 0:w], T.land[:, w:2 * w], accum_op=AluOpType.add).then_inc(sem.added, 16)
-        done += 16
-        g.wait_ge(sem.added, done)
-        w //= 2
-
-    g.dma_start(T.y[:], T.land[:, 0:b]).then_inc(sem.added, 16)
-    done += 16
-    g.wait_ge(sem.added, done)
-    g.wait_ge(sem.sent, engines * (n - 1))
+    g.wait_ge(sem.mine, 16)
+    g.wait_ge(sem.folded, 16)
+    g.dma_start(T.y[:], T.res[:], accum_op=AluOpType.add, max_dma_last_dim=8192).then_inc(sem.mine, 16)
+    g.wait_ge(sem.mine, 32)
+    g.wait_ge(sem.sent, len(others))

from concourse.bass import DstId, RemoteDMATransfer
from concourse.mybir import AluOpType

SCRATCH = {
    "stage": ("dram", [8, 128, 32], "float32"),
    "land": ("dram", [8, 128, 32], "float32"),
    "res": ("dram", [128, 32], "float32"),
}
SEMAPHORES = ["staged", "sent", "arrived", "folded", "mine"]


def helper_of(c):
    return c + 1


def rank_program(g, core, T, topo):
    sem = T.sem
    groups = T.tables["GROUPS"]
    rank = T.rank_of(core)

    if rank is None:
        owner = T.rank_of(core - 1) if core >= 1 else None
        if owner is None or helper_of(core - 1) != core:
            return
        group = [m for m in groups if owner in m][0]
        i = group.index(owner)
        n = len(group)
        g.wait_ge(sem.arrived, n - 1)
        rid, pid, _se = topo.addr(core - 1)
        m = topo.mask(core, core - 1)
        g.remote_dma_fused(
            [RemoteDMATransfer(dst_ids=[DstId(rid=rid, pnc=pid)], dma_engine_mask=m, remote_sem=sem.folded,
                               srcs=[T.land[s] for s in range(n) if s != i], dsts=[T.res[:]], alu_op=1)],
            local_sem=sem.sent)
        g.wait_ge(sem.sent, bin(m).count("1"))
        return

    group = [m for m in groups if rank in m][0]
    n = len(group)
    i = group.index(rank)
    b = T.x.shape[1] // n

    g.dma_start(T.y[:], T.x[:, i * b:(i + 1) * b]).then_inc(sem.mine, 16)
    others = [(i + k) % n for k in range(1, n)]
    for k, j in enumerate(others):
        q = g.sync if k % 2 == 0 else g.scalar
        q.dma_start(T.stage[j], T.x[:, j * b:(j + 1) * b]).then_inc(sem.staged, 16)
    g.wait_ge(sem.staged, 16 * len(others))

    transfers = []
    for k, j in enumerate(others):
        rid, pid, _se = topo.addr(helper_of(T.cores[group[j]]))
        transfers.append(RemoteDMATransfer(dst_ids=[DstId(rid=rid, pnc=pid)], dma_engine_mask=1 << k,
                                           remote_sem=sem.arrived, src=T.stage[j], dst=T.land[i]))
    g.remote_dma_fused(transfers, local_sem=sem.sent)

    g.wait_ge(sem.mine, 16)
    g.wait_ge(sem.folded, 16)
    g.dma_start(T.y[:], T.res[:], accum_op=AluOpType.add, max_dma_last_dim=8192).then_inc(sem.mine, 16)
    g.wait_ge(sem.mine, 32)
    g.wait_ge(sem.sent, len(others))
